import numpy as np
import ml_dtypes


def mxq(x, axis, fmt="e4m3"):
    dtype, down = {"e4m3": (ml_dtypes.float8_e4m3fn, 7), "e5m2": (ml_dtypes.float8_e5m2, 14)}[fmt]
    v = np.moveaxis(np.asarray(x, np.float32).astype(ml_dtypes.bfloat16).astype(np.float64), axis, -1)
    blocks = v.reshape(v.shape[:-1] + (-1, 32))
    amax = np.abs(blocks).max(-1, keepdims=True)
    byte = np.maximum(np.where(amax > 0, np.frexp(amax)[1] - 1 + 127, 0) - down, 1)
    scale = np.exp2(byte - 127.0)
    codes = (blocks / scale).astype(np.float32).astype(dtype).astype(np.float64)
    return np.moveaxis((codes * scale).reshape(v.shape), -1, axis)


WIDE = False


def mx_kscale(k):
    if not WIDE:
        return np.ones(k)
    levels = np.array([10, -10, 5, -5, 0])
    if k % 512:
        return np.exp2(np.random.permutation(np.resize(levels, k // 32))).repeat(32)
    a = np.empty((k // 512, 16))
    for p in range(k // 512):
        a[p, :8] = np.random.permutation(np.resize(levels, 8))
        for g in range(8):
            far = levels[np.abs(levels - a[p, g]) >= 10]
            a[p, g + 8] = far[np.random.randint(len(far))]
    return np.exp2(a.ravel()).repeat(32)


def f64(x):
    return np.asarray(x).astype(np.float64)


def striped(idx):
    return np.tile(idx.reshape(-1, 16).T, (8, 1)).astype(np.uint16)


def unstriped(offs):
    return offs[:16].T.reshape(-1).astype(np.int64)


E2M1 = np.array([0.0, 0.5, 1.0, 1.5, 2.0, 3.0, 4.0, 6.0, -0.0, -0.5, -1.0, -1.5, -2.0, -3.0, -4.0, -6.0])


def pack_weight(w, fmt):
    k, n = w.shape
    w = f64(np.asarray(w, np.float32).astype(ml_dtypes.bfloat16)).reshape(k // 32, 32, n)
    amax = np.abs(w).max(1)
    if fmt == "e4m3":
        byte = np.frexp(amax)[1] - 1 + 127 - 7
    else:
        mant, ex = np.frexp(amax / 6.0)
        byte = np.where(mant > 0.5, ex, ex - 1) + 127
    byte = np.clip(np.where(amax > 0, byte, 1), 1, 254)
    scaled = (w * np.exp2(127.0 - byte)[:, None, :]).reshape(k, n).astype(np.float32)
    by_word = np.ascontiguousarray(scaled.reshape(k // 512, 128, 4, n).transpose(0, 1, 3, 2))
    if fmt == "e4m3":
        words = by_word.astype(ml_dtypes.float8_e4m3fn).view(np.uint8)
    else:
        c = by_word.astype(ml_dtypes.float4_e2m1fn).view(np.uint8) & 0xF
        words = (c[..., 0::2] | (c[..., 1::2] << 4)).reshape(k // 512, 128, 2 * n)
    return np.ascontiguousarray(words), np.ascontiguousarray(byte.astype(np.uint8).reshape(k // 512, 16, n))


def unpack_weight(words, scales, fmt):
    g, _, n = scales.shape
    words = np.ascontiguousarray(words).reshape(g, 128, n, -1)
    if fmt == "e4m3":
        vals = words.view(ml_dtypes.float8_e4m3fn).astype(np.float64)
    else:
        nib = np.empty((g, 128, n, 4), np.uint8)
        nib[..., 0::2] = words & 0xF
        nib[..., 1::2] = words >> 4
        vals = E2M1[nib]
    vals = vals * np.repeat(np.exp2(scales.astype(np.float64) - 127.0), 8, axis=1)[..., None]
    return vals.transpose(0, 1, 3, 2).reshape(g * 512, n)


def gelu(v):
    return 0.5 * v * (1.0 + np.tanh(np.sqrt(2.0 / np.pi) * (v + 0.044715 * v**3)))


K, H, T, S, T3, S2 = 1024, 1024, 2048, 512, 1024, 512

def setup_inputs():
    n = np.random.standard_normal
    s = mx_kscale(K)[:, None]
    u = mx_kscale(H)[:, None]
    tab_words, tab_scales = pack_weight(n((K, T)) * s, "e4m3")
    tab2_words, tab2_scales = pack_weight(n((H, T3)) / np.sqrt(H) / u, "e4m3")
    tab3_words, tab3_scales = pack_weight(n((H, T3)) / np.sqrt(H) / u, "e4m3")
    w4_words, w4_scales = pack_weight(n((K, H)) / np.sqrt(K) / s * u.T, "e2m1")
    w8_words, w8_scales = pack_weight(1.5 * n((K, H)) / np.sqrt(K) / s, "e4m3")
    return {
        "tab_words": tab_words, "tab_scales": tab_scales,
        "tab2_words": tab2_words, "tab2_scales": tab2_scales,
        "tab3_words": tab3_words, "tab3_scales": tab3_scales,
        "offs": striped(np.random.permutation(T)[:S]),
        "offs2": striped(np.random.permutation(T3)[:S2]),
        "offs3": striped(np.random.permutation(T3)[:S2]),
        "w1": (n((K, H)) / np.sqrt(K) / s * u.T).astype(np.float32),
        "w4_words": w4_words, "w4_scales": w4_scales,
        "w8_words": w8_words, "w8_scales": w8_scales,
        "bias": (0.6 * n(H)).astype(np.float32),
        "gain": (np.exp(0.3 * n(H)) * u[:, 0]).astype(np.float32),
        "given": (0.8 * n((S2, S))).astype(np.float32),
    }

def reference(tab_words, tab_scales, tab2_words, tab2_scales, tab3_words, tab3_scales, offs, offs2, offs3,
              w1, w4_words, w4_scales, w8_words, w8_scales, bias, gain, given):
    v = unpack_weight(tab_words, tab_scales, "e4m3")[:, unstriped(offs)]
    v2 = unpack_weight(tab2_words, tab2_scales, "e4m3")[:, unstriped(offs2)]
    v3 = unpack_weight(tab3_words, tab3_scales, "e4m3")[:, unstriped(offs3)]
    w4 = unpack_weight(w4_words, w4_scales, "e2m1")
    w8 = unpack_weight(w8_words, w8_scales, "e4m3")
    h1 = np.maximum(mxq(f64(w1), 0, "e4m3").T @ v, w4.T @ v)
    h2 = f64(gain)[:, None] * np.tanh((w8.T @ v) + f64(bias)[:, None])
    e2 = v2.T @ mxq(h1, 0, "e4m3")
    e3 = v3.T @ mxq(h2, 0, "e4m3")
    return np.minimum(e2, e3 + f64(given))

@@ -1,0 +1,276 @@
+from contextlib import ExitStack
+
+import concourse.mybir as mybir
+
+K, H, T, S, T3, S2 = 1024, 1024, 2048, 512, 1024, 512
+FLOPS = 2 * (3 * K * H * S + 2 * H * S2 * S)
+
+F32 = mybir.dt.float32
+BF16 = mybir.dt.bfloat16
+I32 = mybir.dt.int32
+U32 = mybir.dt.uint32
+U16 = mybir.dt.uint16
+U8 = mybir.dt.uint8
+FP8X4 = mybir.dt.float8_e4m3fn_x4
+FP4X4 = mybir.dt.float4_e2m1fn_x4
+ALU = mybir.AluOpType
+ACT = mybir.ActivationFunctionType
+
+P = 128
+PACK = 4
+PASS = P * PACK
+NPASS = K // PASS
+JW = 128
+
+
+def tile_list_locum_consultant_scores_kernel(
+    tc, tab_words, tab_scales, tab2_words, tab2_scales, tab3_words, tab3_scales, offs, offs2, offs3,
+    w1, w4_words, w4_scales, w8_words, w8_scales, bias, gain, given, out,
+):
+    nc = tc.nc
+    with ExitStack() as ctx:
+        keep = ctx.enter_context(tc.tile_pool(name="keep", bufs=1))
+        ps1 = ctx.enter_context(tc.psum_pool(name="ps1", bufs=4))
+        ps2 = ctx.enter_context(tc.psum_pool(name="ps2", bufs=4))
+
+        def tile(shape, dtype, name):
+            return keep.tile(shape, dtype, name=name, align_bytes=64)
+
+        def words(ap):
+            return ap.rearrange("p n i -> p (n i)").bitcast(I32)
+
+        off1 = keep.tile([P, S // 16], U16, name="off1")
+        off2 = keep.tile([P, S2 // 16], U16, name="off2")
+        off3 = keep.tile([P, S2 // 16], U16, name="off3")
+
+        v_sc = tile([P, NPASS * T], U8, "v_sc")
+        w_sc = tile([P, NPASS * H], U8, "w_sc")
+        v2_sc = tile([P, T3], U8, "v2_sc")
+        v3_sc = tile([P, T3], U8, "v3_sc")
+        nc.gpsimd.memset(v_sc[:, :T].bitcast(I32), 0)
+        nc.vector.memset(v_sc[:, T:].bitcast(I32), 0)
+        nc.vector.memset(w_sc[:].bitcast(I32), 0)
+        nc.gpsimd.memset(v3_sc[:].bitcast(I32), 0)
+        nc.gpsimd.memset(v2_sc[:].bitcast(I32), 0)
+
+        def load_planes_side_by_side(queue, dst, first, scales):
+            for q in range(4):
+                rows = dst[32 * q + first : 32 * q + first + 4, :].bitcast(I32)
+                queue.dma_start(
+                    out=rows.rearrange("r (a n) -> r a n", a=NPASS),
+                    in_=scales[:, 4 * q : 4 * q + 4, :].bitcast(I32).rearrange("a r n -> r a n"),
+                )
+
+        def load_planes_stacked(queue, dst, scales):
+            for q in range(4):
+                queue.dma_start(
+                    out=dst[32 * q : 32 * q + 8, :].bitcast(I32),
+                    in_=scales[:, 4 * q : 4 * q + 4, :].bitcast(I32),
+                )
+
+        v_w = [tile([P, T], U32, f"v_w{a}") for a in range(NPASS)]
+        v2_w = [tile([P, T3], U32, f"v2_w{a}") for a in range(NPASS)]
+        v3_w = [tile([P, T3], U32, f"v3_w{a}") for a in range(NPASS)]
+        w4_raw = tile([P, H], I32, "w4_raw")
+        w8_raw = [tile([P, H], I32, f"w8_raw{a}") for a in range(NPASS)]
+        w1_raw = [[tile([P, PACK, PASS], F32, f"w1_raw{b}{a}") for a in range(NPASS)] for b in range(2)]
+        given_t = tile([P, 4, S], F32, "given_t")
+        bias_t = tile([P, 8], F32, "bias_t")
+        gain_t = tile([P, 8], F32, "gain_t")
+
+        def load_w1(b, a):
+            rows = w1[PASS * a : PASS * (a + 1), PASS * b : PASS * (b + 1)]
+            nc.sync.dma_start(out=w1_raw[b][a][:], in_=rows.rearrange("(p j) c -> p j c", j=PACK))
+
+        def load_words(dst, src):
+            nc.sync.dma_start(out=dst[:].bitcast(I32), in_=words(src))
+
+        def load_vector(dst, src):
+            nc.sync.dma_start(out=dst[:].rearrange("p (b t) -> p b t", t=PACK),
+                              in_=src.rearrange("(b p t) -> p b t", p=P, t=PACK))
+
+        nc.sync.dma_start(off1[:], offs)
+        load_words(v_w[0], tab_words[0])
+        load_planes_side_by_side(nc.sync, v_sc, 0, tab_scales)
+        load_words(v_w[1], tab_words[1])
+        load_planes_side_by_side(nc.sync, w_sc, 0, w4_scales)
+        nc.sync.dma_start(out=w4_raw[:].rearrange("p (a n) -> p a n", a=NPASS),
+                          in_=w4_words.bitcast(I32).rearrange("a p n -> p a n"))
+        load_planes_side_by_side(nc.sync, w_sc, 4, w8_scales)
+        nc.sync.dma_start(out=w8_raw[0][:], in_=words(w8_words[0]))
+        load_vector(bias_t, bias)
+        load_vector(gain_t, gain)
+        nc.sync.dma_start(out=w8_raw[1][:], in_=words(w8_words[1]))
+        nc.sync.dma_start(off3[:], offs3)
+        load_planes_stacked(nc.sync, v3_sc, tab3_scales)
+        load_words(v3_w[0], tab3_words[0])
+        load_words(v3_w[1], tab3_words[1])
+        load_w1(0, 0)
+        nc.sync.dma_start(off2[:], offs2)
+        load_planes_stacked(nc.sync, v2_sc, tab2_scales)
+        load_w1(0, 1)
+        load_words(v2_w[0], tab2_words[0])
+        load_words(v2_w[1], tab2_words[1])
+        load_w1(1, 0)
+        load_w1(1, 1)
+        nc.sync.dma_start(out=given_t[:], in_=given.rearrange("(m p) j -> p m j", p=P))
+
+        g_w = [tile([P, S], U32, f"g_w{a}") for a in range(NPASS)]
+        g_sc = [tile([P, S], U8, f"g_sc{a}") for a in range(NPASS)]
+        w4_d = tile([P, NPASS * H], U16, "w4_d")
+        wd_sc = tile([P, NPASS * H], U8, "wd_sc")
+        w8_d = [tile([P, H], I32, f"w8_d{a}") for a in range(NPASS)]
+        for a in range(NPASS):
+            nc.scalar.copy(
+                out=w4_d[:, H * a : H * (a + 1)].rearrange("p (b t q) -> p b t q", b=2, t=PACK),
+                in_=w4_raw[:, 512 * a : 512 * (a + 1)].bitcast(U16).rearrange("p (b q t) -> p b t q", b=2, t=PACK),
+            )
+        nc.vector.tensor_copy(g_w[0][:], v_w[0][:].indirect(off1[:]))
+        for a in range(NPASS):
+            nc.vector.tensor_copy(g_sc[a][:], v_sc[:, T * a : T * (a + 1)].indirect(off1[:]))
+        nc.vector.tensor_copy(g_w[1][:], v_w[1][:].indirect(off1[:]))
+        nc.vector.tensor_copy(
+            out=wd_sc[:].rearrange("p (g t q) -> p g t q", g=4, t=PACK),
+            in_=w_sc[:].rearrange("p (g q t) -> p g t q", g=4, t=PACK),
+        )
+        for a in range(NPASS):
+            nc.vector.tensor_copy(
+                out=w8_d[a][:].rearrange("p (b t c i) -> p b c t i", b=2, t=PACK, i=4),
+                in_=w8_raw[a][:].rearrange("p (b c i t) -> p b c t i", b=2, t=PACK, i=4),
+            )
+
+        def gather_candidates(name, src_w, src_sc, off):
+            c_w = [tile([P, S2], U32, f"{name}_w{a}") for a in range(NPASS)]
+            c_sc = tile([P, S2], U8, f"{name}_sc")
+            nc.vector.tensor_copy(c_sc[:], src_sc[:].indirect(off[:]))
+            for a in range(NPASS):
+                nc.vector.tensor_copy(c_w[a][:], src_w[a][:].indirect(off[:]))
+            return c_w, c_sc
+
+        def cols(b, t):
+            return slice(PASS * b + P * t, PASS * b + P * (t + 1))
+
+        p4 = [tile([P, PACK * S], F32, f"p4_{b}") for b in range(2)]
+
+        def product_w4(b):
+            for jc in range(S // JW):
+                js = slice(JW * jc, JW * (jc + 1))
+                bank = ps1.tile([P, PACK, JW], F32, name="bank1")
+                for t in range(PACK):
+                    for a in range(NPASS):
+                        c = cols(b, t)
+                        ca = slice(H * a + c.start, H * a + c.stop)
+                        nc.tensor.matmul_mx(
+                            out=bank[:, t, :], lhsT=w4_d[:, ca].bitcast(FP4X4), lhsT_scale=wd_sc[:, ca],
+                            rhs=g_w[a][:, js].bitcast(FP8X4), rhs_scale=g_sc[a][:, js],
+                            start=(a == 0), stop=(a == NPASS - 1),
+                        )
+                nc.scalar.copy(
+                    out=p4[b][:, PASS * jc : PASS * (jc + 1)].rearrange("p (j t) -> p j t", t=PACK),
+                    in_=bank[:].rearrange("p t j -> p j t"),
+                )
+
+        th = [tile([P, PACK, S], F32, f"th{b}") for b in range(2)]
+        h2_bf = [tile([P, PACK * S], BF16, f"h2_bf{b}") for b in range(2)]
+        h2_w = [tile([P, S], U32, f"h2_w{b}") for b in range(2)]
+        h2_sc = [tile([P, S], U8, f"h2_sc{b}") for b in range(2)]
+
+        def product_w8(b):
+            for t in range(PACK):
+                bank = ps1.tile([P, PACK, JW], F32, name="bank1")
+                flat = bank[:].rearrange("p t j -> p (t j)")
+                for a in range(NPASS):
+                    c = cols(b, t)
+                    ca = slice(H * a + c.start, H * a + c.stop)
+                    nc.tensor.matmul_mx(
+                        out=flat, lhsT=w8_d[a][:, c].bitcast(FP8X4), lhsT_scale=wd_sc[4:P, ca],
+                        rhs=g_w[a][:].bitcast(FP8X4), rhs_scale=g_sc[a][:],
+                        start=(a == 0), stop=(a == NPASS - 1),
+                    )
+                nc.scalar.activation(out=th[b][:, t, :], in_=flat, func=ACT.Tanh,
+                                     bias=bias_t[:, PACK * b + t : PACK * b + t + 1])
+
+        def make_h2(b):
+            g = gain_t[:, PACK * b : PACK * (b + 1)].unsqueeze(1).unsqueeze(3).to_broadcast([P, S // 4, PACK, 4])
+            nc.vector.tensor_tensor(
+                out=h2_bf[b][:].rearrange("p (c i t) -> p c t i", i=4, t=PACK),
+                in0=th[b][:].rearrange("p t (c i) -> p c t i", i=4),
+                in1=g, op=ALU.mult,
+            )
+
+        def quantise(codes, scales, src):
+            nc.vector.quantize_mx(out=codes.bitcast(FP8X4), scales=scales, in_=src)
+
+        w1_bf = [[tile([P, PACK * PASS], BF16, f"w1_bf{b}{a}") for a in range(NPASS)] for b in range(2)]
+        w1_w = [[tile([P, PASS], U32, f"w1_w{b}{a}") for a in range(NPASS)] for b in range(2)]
+        w1_sc = [[tile([P, PASS], U8, f"w1_sc{b}{a}") for a in range(NPASS)] for b in range(2)]
+
+        def round_w1(b, a):
+            nc.scalar.copy(
+                out=w1_bf[b][a][:].rearrange("p (t q j) -> p q j t", t=PACK, j=PACK),
+                in_=w1_raw[b][a][:].rearrange("p j (q t) -> p q j t", t=PACK),
+            )
+            quantise(w1_w[b][a][:], w1_sc[b][a][:], w1_bf[b][a][:])
+
+        h1_bf = [tile([P, PACK * S], BF16, f"h1_bf{b}") for b in range(2)]
+        h1_w = [tile([P, S], U32, f"h1_w{b}") for b in range(2)]
+        h1_sc = [tile([P, S], U8, f"h1_sc{b}") for b in range(2)]
+
+        def make_h1(b):
+            for jc in range(S // JW):
+                js = slice(JW * jc, JW * (jc + 1))
+                bank = ps1.tile([P, PACK, JW], F32, name="bank1")
+                for t in range(PACK):
+                    ts = slice(P * t, P * (t + 1))
+                    for a in range(NPASS):
+                        nc.tensor.matmul_mx(
+                            out=bank[:, t, :], lhsT=w1_w[b][a][:, ts].bitcast(FP8X4), lhsT_scale=w1_sc[b][a][:, ts],
+                            rhs=g_w[a][:, js].bitcast(FP8X4), rhs_scale=g_sc[a][:, js],
+                            start=(a == 0), stop=(a == NPASS - 1),
+                        )
+                part = slice(PASS * jc, PASS * (jc + 1))
+                nc.vector.tensor_tensor(
+                    out=h1_bf[b][:, part].rearrange("p (j t) -> p j t", t=PACK),
+                    in0=bank[:].rearrange("p t j -> p j t"),
+                    in1=p4[b][:, part].rearrange("p (j t) -> p j t", t=PACK),
+                    op=ALU.max,
+                )
+            quantise(h1_w[b][:], h1_sc[b][:], h1_bf[b][:])
+
+        def scores(c_w, c_sc, h_w, h_sc):
+            banks = [ps2.tile([P, S], F32, name="bank2") for m in range(S2 // P)]
+            for b in range(2):
+                for m in range(S2 // P):
+                    ms = slice(P * m, P * (m + 1))
+                    nc.tensor.matmul_mx(
+                        out=banks[m][:], lhsT=c_w[b][:, ms].bitcast(FP8X4), lhsT_scale=c_sc[4 * b : P, ms],
+                        rhs=h_w[b][:].bitcast(FP8X4), rhs_scale=h_sc[b][:],
+                        start=(b == 0), stop=(b == 1),
+                    )
+            return banks
+
+        product_w8(0)
+        product_w8(1)
+        c3_w, c3_sc = gather_candidates("c3", v3_w, v3_sc, off3)
+        make_h2(0)
+        round_w1(0, 0)
+        make_h2(1)
+        quantise(h2_w[0][:], h2_sc[0][:], h2_bf[0][:])
+        product_w4(0)
+        round_w1(0, 1)
+        quantise(h2_w[1][:], h2_sc[1][:], h2_bf[1][:])
+        c2_w, c2_sc = gather_candidates("c2", v2_w, v2_sc, off2)
+        make_h1(0)
+        round_w1(1, 0)
+        product_w4(1)
+        round_w1(1, 1)
+        e3 = scores(c3_w, c3_sc, h2_w, h2_sc)
+        shifted = [tile([P, S], F32, f"shifted{m}") for m in range(S2 // P)]
+        make_h1(1)
+        for m in range(S2 // P):
+            nc.vector.tensor_tensor(out=shifted[m][:], in0=e3[m][:], in1=given_t[:, m, :], op=ALU.add)
+        e2 = scores(c2_w, c2_sc, h1_w, h1_sc)
+        for m in range(S2 // P):
+            res = tile([P, S], F32, f"res{m}")
+            nc.vector.tensor_tensor(out=res[:], in0=e2[m][:], in1=shifted[m][:], op=ALU.min)
+            nc.sync.dma_start(out=out[P * m : P * (m + 1), :], in_=res[:])

@@ -30,11 +30,12 @@ def tile_list_locum_consultant_scores_kernel(
     nc = tc.nc
     with ExitStack() as ctx:
         keep = ctx.enter_context(tc.tile_pool(name="keep", bufs=1))
-        ps1 = ctx.enter_context(tc.psum_pool(name="ps1", bufs=4))
-        ps2 = ctx.enter_context(tc.psum_pool(name="ps2", bufs=4))
+        psum = ctx.enter_context(tc.psum_pool(name="psum", bufs=1))
+        low = [psum.tile([P, S], F32, name=f"low{i}") for i in range(4)]
+        high = [psum.tile([P, S], F32, name=f"high{i}") for i in range(4)]
 
-        def tile(shape, dtype, name):
-            return keep.tile(shape, dtype, name=name, align_bytes=64)
+        def tile(shape, dtype, name, tag=None):
+            return keep.tile(shape, dtype, name=name, tag=tag or name, align_bytes=64)
 
         def words(ap):
             return ap.rearrange("p n i -> p (n i)").bitcast(I32)
@@ -43,131 +44,135 @@ def tile_list_locum_consultant_scores_kernel(
         off2 = keep.tile([P, S2 // 16], U16, name="off2")
         off3 = keep.tile([P, S2 // 16], U16, name="off3")
 
-        v_sc = tile([P, NPASS * T], U8, "v_sc")
-        w_sc = tile([P, NPASS * H], U8, "w_sc")
+        v_sc = tile([P, T], U8, "v_sc")
+        w_sc = tile([P, H], U8, "w_sc")
         v2_sc = tile([P, T3], U8, "v2_sc")
         v3_sc = tile([P, T3], U8, "v3_sc")
-        nc.gpsimd.memset(v_sc[:, :T].bitcast(I32), 0)
-        nc.vector.memset(v_sc[:, T:].bitcast(I32), 0)
-        nc.vector.memset(w_sc[:].bitcast(I32), 0)
+        g_sc_low = tile([P, S], U8, "g_sc_low")
+        w4_sc = [tile([P, H], U8, f"w4_sc{a}") for a in range(NPASS)]
         nc.gpsimd.memset(v3_sc[:].bitcast(I32), 0)
-        nc.gpsimd.memset(v2_sc[:].bitcast(I32), 0)
+        nc.gpsimd.memset(v_sc[:].bitcast(I32), 0)
+        nc.vector.memset(w_sc[:].bitcast(I32), 0)
+        nc.vector.memset(v2_sc[:].bitcast(I32), 0)
+        nc.gpsimd.memset(g_sc_low[:].bitcast(I32), 0)
+        for a in range(NPASS):
+            nc.gpsimd.memset(w4_sc[a][:].bitcast(I32), 0)
 
-        def load_planes_side_by_side(queue, dst, first, scales):
+        def load_planes(dst, first, scales):
             for q in range(4):
-                rows = dst[32 * q + first : 32 * q + first + 4, :].bitcast(I32)
-                queue.dma_start(
-                    out=rows.rearrange("r (a n) -> r a n", a=NPASS),
-                    in_=scales[:, 4 * q : 4 * q + 4, :].bitcast(I32).rearrange("a r n -> r a n"),
-                )
-
-        def load_planes_stacked(queue, dst, scales):
-            for q in range(4):
-                queue.dma_start(
-                    out=dst[32 * q : 32 * q + 8, :].bitcast(I32),
+                nc.sync.dma_start(
+                    out=dst[32 * q + first : 32 * q + first + 8, :].bitcast(I32),
                     in_=scales[:, 4 * q : 4 * q + 4, :].bitcast(I32),
                 )
 
+        def lower_plane(dst, src, first):
+            nc.sync.dma_start(out=dst[0:100, :].bitcast(I32), in_=src[first : first + 100, :].bitcast(I32))
+
         v_w = [tile([P, T], U32, f"v_w{a}") for a in range(NPASS)]
-        v2_w = [tile([P, T3], U32, f"v2_w{a}") for a in range(NPASS)]
-        v3_w = [tile([P, T3], U32, f"v3_w{a}") for a in range(NPASS)]
+        v3_all = tile([P, NPASS * T3], U32, "v3_all")
+        v2_all = tile([P, NPASS * T3], U32, "v2_all")
+        v3_w = [v3_all[:, T3 * a : T3 * (a + 1)] for a in range(NPASS)]
+        v2_w = [v2_all[:, T3 * a : T3 * (a + 1)] for a in range(NPASS)]
         w4_raw = tile([P, H], I32, "w4_raw")
-        w8_raw = [tile([P, H], I32, f"w8_raw{a}") for a in range(NPASS)]
-        w1_raw = [[tile([P, PACK, PASS], F32, f"w1_raw{b}{a}") for a in range(NPASS)] for b in range(2)]
-        given_t = tile([P, 4, S], F32, "given_t")
+        w8_raw = [tile([P, H], U32, f"w8_raw{a}") for a in range(NPASS)]
+        w1_raw = {}
         bias_t = tile([P, 8], F32, "bias_t")
         gain_t = tile([P, 8], F32, "gain_t")
 
         def load_w1(b, a):
             rows = w1[PASS * a : PASS * (a + 1), PASS * b : PASS * (b + 1)]
-            nc.sync.dma_start(out=w1_raw[b][a][:], in_=rows.rearrange("(p j) c -> p j c", j=PACK))
+            w1_raw[b, a] = tile([P, PACK, PASS], F32, f"w1_raw{b}{a}", (None, "w_sc", "v3_all", "w4_raw")[2 * b + a])
+            nc.sync.dma_start(out=w1_raw[b, a][:], in_=rows.rearrange("(p j) c -> p j c", j=PACK))
 
         def load_words(dst, src):
-            nc.sync.dma_start(out=dst[:].bitcast(I32), in_=words(src))
+            nc.sync.dma_start(out=dst.bitcast(I32), in_=words(src))
 
         def load_vector(dst, src):
             nc.sync.dma_start(out=dst[:].rearrange("p (b t) -> p b t", t=PACK),
                               in_=src.rearrange("(b p t) -> p b t", p=P, t=PACK))
 
         nc.sync.dma_start(off1[:], offs)
-        load_words(v_w[0], tab_words[0])
-        load_planes_side_by_side(nc.sync, v_sc, 0, tab_scales)
-        load_words(v_w[1], tab_words[1])
-        load_planes_side_by_side(nc.sync, w_sc, 0, w4_scales)
+        load_words(v_w[0][:], tab_words[0])
+        nc.sync.dma_start(off3[:], offs3)
+        load_planes(v3_sc, 0, tab3_scales)
+        load_words(w8_raw[0][:], w8_words[0])
+        load_planes(v_sc, 0, tab_scales)
+        load_words(v_w[1][:], tab_words[1])
+        load_planes(w_sc, 0, w8_scales)
+        load_words(w8_raw[1][:], w8_words[1])
+        load_planes(w_sc, 8, w4_scales)
+        load_words(v3_w[0], tab3_words[0])
+        nc.sync.dma_start(off2[:], offs2)
+        load_planes(v2_sc, 0, tab2_scales)
+        load_vector(bias_t, bias)
         nc.sync.dma_start(out=w4_raw[:].rearrange("p (a n) -> p a n", a=NPASS),
                           in_=w4_words.bitcast(I32).rearrange("a p n -> p a n"))
-        load_planes_side_by_side(nc.sync, w_sc, 4, w8_scales)
-        nc.sync.dma_start(out=w8_raw[0][:], in_=words(w8_words[0]))
-        load_vector(bias_t, bias)
-        load_vector(gain_t, gain)
-        nc.sync.dma_start(out=w8_raw[1][:], in_=words(w8_words[1]))
-        nc.sync.dma_start(off3[:], offs3)
-        load_planes_stacked(nc.sync, v3_sc, tab3_scales)
-        load_words(v3_w[0], tab3_words[0])
         load_words(v3_w[1], tab3_words[1])
-        load_w1(0, 0)
-        nc.sync.dma_start(off2[:], offs2)
-        load_planes_stacked(nc.sync, v2_sc, tab2_scales)
-        load_w1(0, 1)
+        load_vector(gain_t, gain)
         load_words(v2_w[0], tab2_words[0])
         load_words(v2_w[1], tab2_words[1])
-        load_w1(1, 0)
-        load_w1(1, 1)
-        nc.sync.dma_start(out=given_t[:], in_=given.rearrange("(m p) j -> p m j", p=P))
+        load_w1(0, 0)
 
         g_w = [tile([P, S], U32, f"g_w{a}") for a in range(NPASS)]
-        g_sc = [tile([P, S], U8, f"g_sc{a}") for a in range(NPASS)]
+        g_sc = tile([P, S], U8, "g_sc")
         w4_d = tile([P, NPASS * H], U16, "w4_d")
-        wd_sc = tile([P, NPASS * H], U8, "wd_sc")
-        w8_d = [tile([P, H], I32, f"w8_d{a}") for a in range(NPASS)]
-        for a in range(NPASS):
+        wd_sc = tile([P, H], U8, "wd_sc")
+        w8_d = [tile([P, H], U32, f"w8_d{a}", f"stage{a}") for a in range(NPASS)]
+
+        def deal_w8(a):
             nc.scalar.copy(
-                out=w4_d[:, H * a : H * (a + 1)].rearrange("p (b t q) -> p b t q", b=2, t=PACK),
-                in_=w4_raw[:, 512 * a : 512 * (a + 1)].bitcast(U16).rearrange("p (b q t) -> p b t q", b=2, t=PACK),
-            )
-        nc.vector.tensor_copy(g_w[0][:], v_w[0][:].indirect(off1[:]))
-        for a in range(NPASS):
-            nc.vector.tensor_copy(g_sc[a][:], v_sc[:, T * a : T * (a + 1)].indirect(off1[:]))
-        nc.vector.tensor_copy(g_w[1][:], v_w[1][:].indirect(off1[:]))
-        nc.vector.tensor_copy(
-            out=wd_sc[:].rearrange("p (g t q) -> p g t q", g=4, t=PACK),
-            in_=w_sc[:].rearrange("p (g q t) -> p g t q", g=4, t=PACK),
-        )
-        for a in range(NPASS):
-            nc.vector.tensor_copy(
                 out=w8_d[a][:].rearrange("p (b t c i) -> p b c t i", b=2, t=PACK, i=4),
                 in_=w8_raw[a][:].rearrange("p (b c i t) -> p b c t i", b=2, t=PACK, i=4),
             )
 
-        def gather_candidates(name, src_w, src_sc, off):
-            c_w = [tile([P, S2], U32, f"{name}_w{a}") for a in range(NPASS)]
-            c_sc = tile([P, S2], U8, f"{name}_sc")
-            nc.vector.tensor_copy(c_sc[:], src_sc[:].indirect(off[:]))
-            for a in range(NPASS):
-                nc.vector.tensor_copy(c_w[a][:], src_w[a][:].indirect(off[:]))
-            return c_w, c_sc
+        def deal_w4(a):
+            nc.scalar.copy(
+                out=w4_d[:, H * a : H * (a + 1)].rearrange("p (b t q) -> p b t q", b=2, t=PACK),
+                in_=w4_raw[:, 512 * a : 512 * (a + 1)].bitcast(U16).rearrange("p (b q t) -> p b t q", b=2, t=PACK),
+            )
+
+        deal_w8(0)
+        deal_w8(1)
+        deal_w4(0)
+        deal_w4(1)
+        nc.vector.tensor_copy(g_w[0][:], v_w[0][:].indirect(off1[:]))
+        nc.vector.tensor_copy(g_sc[:], v_sc[:].indirect(off1[:]))
+        lower_plane(g_sc_low, g_sc, 4)
+        nc.vector.tensor_copy(g_w[1][:], v_w[1][:].indirect(off1[:]))
+        nc.vector.tensor_copy(
+            out=wd_sc[:].rearrange("p (b t q) -> p b t q", b=2, t=PACK),
+            in_=w_sc[:].rearrange("p (b q t) -> p b t q", b=2, t=PACK),
+        )
+        for a in range(NPASS):
+            lower_plane(w4_sc[a], wd_sc, 8 + 4 * a)
+
+        def gather(name, dtype, window, off, tag=None):
+            picked = tile([P, S2], dtype, name, tag)
+            nc.vector.tensor_copy(picked[:], window.indirect(off[:]))
+            return picked
 
         def cols(b, t):
             return slice(PASS * b + P * t, PASS * b + P * (t + 1))
 
-        p4 = [tile([P, PACK * S], F32, f"p4_{b}") for b in range(2)]
+        p4 = {}
 
-        def product_w4(b):
+        def product_w4(b, banks):
+            p4[b] = tile([P, PACK * S], F32, f"p4_{b}", (None, "w4_raw")[b])
             for jc in range(S // JW):
                 js = slice(JW * jc, JW * (jc + 1))
-                bank = ps1.tile([P, PACK, JW], F32, name="bank1")
+                bank = banks[jc][:].rearrange("p (t j) -> p t j", t=PACK)
                 for t in range(PACK):
                     for a in range(NPASS):
                         c = cols(b, t)
                         ca = slice(H * a + c.start, H * a + c.stop)
                         nc.tensor.matmul_mx(
-                            out=bank[:, t, :], lhsT=w4_d[:, ca].bitcast(FP4X4), lhsT_scale=wd_sc[:, ca],
-                            rhs=g_w[a][:, js].bitcast(FP8X4), rhs_scale=g_sc[a][:, js],
+                            out=bank[:, t, :], lhsT=w4_d[:, ca].bitcast(FP4X4), lhsT_scale=w4_sc[a][:, c],
+                            rhs=g_w[a][:, js].bitcast(FP8X4), rhs_scale=(g_sc, g_sc_low)[a][:, js],
                             start=(a == 0), stop=(a == NPASS - 1),
                         )
                 nc.scalar.copy(
                     out=p4[b][:, PASS * jc : PASS * (jc + 1)].rearrange("p (j t) -> p j t", t=PACK),
-                    in_=bank[:].rearrange("p t j -> p j t"),
+                    in_=bank.rearrange("p t j -> p j t"),
                 )
 
         th = [tile([P, PACK, S], F32, f"th{b}") for b in range(2)]
@@ -175,16 +180,14 @@ def tile_list_locum_consultant_scores_kernel(
         h2_w = [tile([P, S], U32, f"h2_w{b}") for b in range(2)]
         h2_sc = [tile([P, S], U8, f"h2_sc{b}") for b in range(2)]
 
-        def product_w8(b):
+        def product_w8(b, banks):
             for t in range(PACK):
-                bank = ps1.tile([P, PACK, JW], F32, name="bank1")
-                flat = bank[:].rearrange("p t j -> p (t j)")
+                flat = banks[t][:]
                 for a in range(NPASS):
                     c = cols(b, t)
-                    ca = slice(H * a + c.start, H * a + c.stop)
                     nc.tensor.matmul_mx(
-                        out=flat, lhsT=w8_d[a][:, c].bitcast(FP8X4), lhsT_scale=wd_sc[4:P, ca],
-                        rhs=g_w[a][:].bitcast(FP8X4), rhs_scale=g_sc[a][:],
+                        out=flat, lhsT=w8_d[a][:, c].bitcast(FP8X4), lhsT_scale=wd_sc[4 * a : P, c],
+                        rhs=g_w[a][:].bitcast(FP8X4), rhs_scale=g_sc[4 * a : P, :],
                         start=(a == 0), stop=(a == NPASS - 1),
                     )
                 nc.scalar.activation(out=th[b][:, t, :], in_=flat, func=ACT.Tanh,
@@ -201,44 +204,45 @@ def tile_list_locum_consultant_scores_kernel(
         def quantise(codes, scales, src):
             nc.vector.quantize_mx(out=codes.bitcast(FP8X4), scales=scales, in_=src)
 
-        w1_bf = [[tile([P, PACK * PASS], BF16, f"w1_bf{b}{a}") for a in range(NPASS)] for b in range(2)]
         w1_w = [[tile([P, PASS], U32, f"w1_w{b}{a}") for a in range(NPASS)] for b in range(2)]
         w1_sc = [[tile([P, PASS], U8, f"w1_sc{b}{a}") for a in range(NPASS)] for b in range(2)]
 
         def round_w1(b, a):
-            nc.scalar.copy(
-                out=w1_bf[b][a][:].rearrange("p (t q j) -> p q j t", t=PACK, j=PACK),
-                in_=w1_raw[b][a][:].rearrange("p j (q t) -> p q j t", t=PACK),
-            )
-            quantise(w1_w[b][a][:], w1_sc[b][a][:], w1_bf[b][a][:])
+            rounded = tile([P, PACK * PASS], BF16, f"w1_bf{b}{a}", "stage0" if (b, a) == (0, 0) else None)
+            dst = rounded[:].rearrange("p (t q j) -> p q j t", t=PACK, j=PACK)
+            src = w1_raw[b, a][:].rearrange("p j (q t) -> p q j t", t=PACK)
+            if (b, a) == (0, 1):
+                nc.vector.tensor_copy(out=dst, in_=src)
+            else:
+                nc.scalar.copy(out=dst, in_=src)
+            quantise(w1_w[b][a][:], w1_sc[b][a][:], rounded[:])
 
         h1_bf = [tile([P, PACK * S], BF16, f"h1_bf{b}") for b in range(2)]
         h1_w = [tile([P, S], U32, f"h1_w{b}") for b in range(2)]
         h1_sc = [tile([P, S], U8, f"h1_sc{b}") for b in range(2)]
 
-        def make_h1(b):
+        def make_h1(b, banks):
             for jc in range(S // JW):
                 js = slice(JW * jc, JW * (jc + 1))
-                bank = ps1.tile([P, PACK, JW], F32, name="bank1")
+                bank = banks[jc][:].rearrange("p (t j) -> p t j", t=PACK)
                 for t in range(PACK):
                     ts = slice(P * t, P * (t + 1))
                     for a in range(NPASS):
                         nc.tensor.matmul_mx(
                             out=bank[:, t, :], lhsT=w1_w[b][a][:, ts].bitcast(FP8X4), lhsT_scale=w1_sc[b][a][:, ts],
-                            rhs=g_w[a][:, js].bitcast(FP8X4), rhs_scale=g_sc[a][:, js],
+                            rhs=g_w[a][:, js].bitcast(FP8X4), rhs_scale=g_sc[4 * a : P, js],
                             start=(a == 0), stop=(a == NPASS - 1),
                         )
                 part = slice(PASS * jc, PASS * (jc + 1))
                 nc.vector.tensor_tensor(
                     out=h1_bf[b][:, part].rearrange("p (j t) -> p j t", t=PACK),
-                    in0=bank[:].rearrange("p t j -> p j t"),
+                    in0=bank.rearrange("p t j -> p j t"),
                     in1=p4[b][:, part].rearrange("p (j t) -> p j t", t=PACK),
                     op=ALU.max,
                 )
             quantise(h1_w[b][:], h1_sc[b][:], h1_bf[b][:])
 
-        def scores(c_w, c_sc, h_w, h_sc):
-            banks = [ps2.tile([P, S], F32, name="bank2") for m in range(S2 // P)]
+        def scores(banks, c_w, c_sc, h_w, h_sc):
             for b in range(2):
                 for m in range(S2 // P):
                     ms = slice(P * m, P * (m + 1))
@@ -249,27 +253,35 @@ def tile_list_locum_consultant_scores_kernel(
                     )
             return banks
 
-        product_w8(0)
-        product_w8(1)
-        c3_w, c3_sc = gather_candidates("c3", v3_w, v3_sc, off3)
+        load_w1(0, 1)
+        product_w8(0, low)
+        product_w8(1, high)
+        c3_sc = gather("c3_sc", U8, v3_sc[:], off3)
+        c3_w = [gather(f"c3_w{a}", U32, v3_w[a], off3) for a in range(NPASS)]
+        c2_sc = gather("c2_sc", U8, v2_sc[:], off2)
+        load_w1(1, 0)
+        load_w1(1, 1)
         make_h2(0)
         round_w1(0, 0)
+        product_w4(0, low)
+        given_t = tile([P, 4, S], F32, "given_t", "w1_raw00")
+        nc.sync.dma_start(out=given_t[:], in_=given.rearrange("(m p) j -> p m j", p=P))
         make_h2(1)
         quantise(h2_w[0][:], h2_sc[0][:], h2_bf[0][:])
-        product_w4(0)
         round_w1(0, 1)
         quantise(h2_w[1][:], h2_sc[1][:], h2_bf[1][:])
-        c2_w, c2_sc = gather_candidates("c2", v2_w, v2_sc, off2)
-        make_h1(0)
+        c2_w0 = gather("c2_w0", U32, v2_w[0], off2, "stage0")
+        make_h1(0, high)
         round_w1(1, 0)
-        product_w4(1)
         round_w1(1, 1)
-        e3 = scores(c3_w, c3_sc, h2_w, h2_sc)
+        c2_w = [c2_w0, gather("c2_w1", U32, v2_w[1], off2, "w1_bf11")]
+        product_w4(1, low)
+        make_h1(1, high)
+        e3 = scores(low, c3_w, c3_sc, h2_w, h2_sc)
         shifted = [tile([P, S], F32, f"shifted{m}") for m in range(S2 // P)]
-        make_h1(1)
         for m in range(S2 // P):
             nc.vector.tensor_tensor(out=shifted[m][:], in0=e3[m][:], in1=given_t[:, m, :], op=ALU.add)
-        e2 = scores(c2_w, c2_sc, h1_w, h1_sc)
+        e2 = scores(high, c2_w, c2_sc, h1_w, h1_sc)
         for m in range(S2 // P):
             res = tile([P, S], F32, f"res{m}")
             nc.vector.tensor_tensor(out=res[:], in0=e2[m][:], in1=shifted[m][:], op=ALU.min)

@@ -45,24 +45,29 @@ def tile_list_locum_consultant_scores_kernel(
         off3 = keep.tile([P, S2 // 16], U16, name="off3")
 
         v_sc = tile([P, T], U8, "v_sc")
-        w_sc = tile([P, H], U8, "w_sc")
+        w_sc = tile([P, NPASS * H], U8, "w_sc")
         v2_sc = tile([P, T3], U8, "v2_sc")
         v3_sc = tile([P, T3], U8, "v3_sc")
         g_sc_low = tile([P, S], U8, "g_sc_low")
-        w4_sc = [tile([P, H], U8, f"w4_sc{a}") for a in range(NPASS)]
-        nc.gpsimd.memset(v3_sc[:].bitcast(I32), 0)
         nc.gpsimd.memset(v_sc[:].bitcast(I32), 0)
         nc.vector.memset(w_sc[:].bitcast(I32), 0)
+        nc.vector.memset(v3_sc[:].bitcast(I32), 0)
         nc.vector.memset(v2_sc[:].bitcast(I32), 0)
-        nc.gpsimd.memset(g_sc_low[:].bitcast(I32), 0)
-        for a in range(NPASS):
-            nc.gpsimd.memset(w4_sc[a][:].bitcast(I32), 0)
+        nc.vector.memset(g_sc_low[:].bitcast(I32), 0)
 
-        def load_planes(dst, first, scales):
+        def load_planes(queue, dst, scales):
             for q in range(4):
-                nc.sync.dma_start(
-                    out=dst[32 * q + first : 32 * q + first + 8, :].bitcast(I32),
+                queue.dma_start(
+                    out=dst[32 * q : 32 * q + 8, :].bitcast(I32),
                     in_=scales[:, 4 * q : 4 * q + 4, :].bitcast(I32),
+                )
+
+        def load_planes_side_by_side(dst, first, scales):
+            for q in range(4):
+                rows = dst[32 * q + first : 32 * q + first + 4, :].bitcast(I32)
+                nc.sync.dma_start(
+                    out=rows.rearrange("r (a n) -> r a n", a=NPASS),
+                    in_=scales[:, 4 * q : 4 * q + 4, :].bitcast(I32).rearrange("a r n -> r a n"),
                 )
 
         def lower_plane(dst, src, first):
@@ -70,9 +75,8 @@ def tile_list_locum_consultant_scores_kernel(
 
         v_w = [tile([P, T], U32, f"v_w{a}") for a in range(NPASS)]
         v3_all = tile([P, NPASS * T3], U32, "v3_all")
-        v2_all = tile([P, NPASS * T3], U32, "v2_all")
         v3_w = [v3_all[:, T3 * a : T3 * (a + 1)] for a in range(NPASS)]
-        v2_w = [v2_all[:, T3 * a : T3 * (a + 1)] for a in range(NPASS)]
+        v2_w0 = tile([P, T3], U32, "v2_w0")
         w4_raw = tile([P, H], I32, "w4_raw")
         w8_raw = [tile([P, H], U32, f"w8_raw{a}") for a in range(NPASS)]
         w1_raw = {}
@@ -91,32 +95,32 @@ def tile_list_locum_consultant_scores_kernel(
             nc.sync.dma_start(out=dst[:].rearrange("p (b t) -> p b t", t=PACK),
                               in_=src.rearrange("(b p t) -> p b t", p=P, t=PACK))
 
+        load_planes(nc.gpsimd, v_sc, tab_scales)
+        load_planes(nc.gpsimd, v2_sc, tab2_scales)
+
         nc.sync.dma_start(off1[:], offs)
         load_words(v_w[0][:], tab_words[0])
-        nc.sync.dma_start(off3[:], offs3)
-        load_planes(v3_sc, 0, tab3_scales)
+        load_planes_side_by_side(w_sc, 4, w8_scales)
         load_words(w8_raw[0][:], w8_words[0])
-        load_planes(v_sc, 0, tab_scales)
+        load_planes_side_by_side(w_sc, 0, w4_scales)
         load_words(v_w[1][:], tab_words[1])
-        load_planes(w_sc, 0, w8_scales)
         load_words(w8_raw[1][:], w8_words[1])
-        load_planes(w_sc, 8, w4_scales)
-        load_words(v3_w[0], tab3_words[0])
-        nc.sync.dma_start(off2[:], offs2)
-        load_planes(v2_sc, 0, tab2_scales)
+        nc.sync.dma_start(off3[:], offs3)
         load_vector(bias_t, bias)
+        load_words(v3_w[0], tab3_words[0])
+        load_planes(nc.sync, v3_sc, tab3_scales)
         nc.sync.dma_start(out=w4_raw[:].rearrange("p (a n) -> p a n", a=NPASS),
                           in_=w4_words.bitcast(I32).rearrange("a p n -> p a n"))
         load_words(v3_w[1], tab3_words[1])
         load_vector(gain_t, gain)
-        load_words(v2_w[0], tab2_words[0])
-        load_words(v2_w[1], tab2_words[1])
+        nc.sync.dma_start(off2[:], offs2)
         load_w1(0, 0)
+        load_words(v2_w0[:], tab2_words[0])
 
         g_w = [tile([P, S], U32, f"g_w{a}") for a in range(NPASS)]
         g_sc = tile([P, S], U8, "g_sc")
         w4_d = tile([P, NPASS * H], U16, "w4_d")
-        wd_sc = tile([P, H], U8, "wd_sc")
+        wd_sc = tile([P, NPASS * H], U8, "wd_sc")
         w8_d = [tile([P, H], U32, f"w8_d{a}", f"stage{a}") for a in range(NPASS)]
 
         def deal_w8(a):
@@ -133,18 +137,14 @@ def tile_list_locum_consultant_scores_kernel(
 
         deal_w8(0)
         deal_w8(1)
-        deal_w4(0)
-        deal_w4(1)
         nc.vector.tensor_copy(g_w[0][:], v_w[0][:].indirect(off1[:]))
+        nc.vector.tensor_copy(
+            out=wd_sc[:].rearrange("p (g t q) -> p g t q", g=4, t=PACK),
+            in_=w_sc[:].rearrange("p (g q t) -> p g t q", g=4, t=PACK),
+        )
         nc.vector.tensor_copy(g_sc[:], v_sc[:].indirect(off1[:]))
         lower_plane(g_sc_low, g_sc, 4)
         nc.vector.tensor_copy(g_w[1][:], v_w[1][:].indirect(off1[:]))
-        nc.vector.tensor_copy(
-            out=wd_sc[:].rearrange("p (b t q) -> p b t q", b=2, t=PACK),
-            in_=w_sc[:].rearrange("p (b q t) -> p b t q", b=2, t=PACK),
-        )
-        for a in range(NPASS):
-            lower_plane(w4_sc[a], wd_sc, 8 + 4 * a)
 
         def gather(name, dtype, window, off, tag=None):
             picked = tile([P, S2], dtype, name, tag)
@@ -166,7 +166,7 @@ def tile_list_locum_consultant_scores_kernel(
                         c = cols(b, t)
                         ca = slice(H * a + c.start, H * a + c.stop)
                         nc.tensor.matmul_mx(
-                            out=bank[:, t, :], lhsT=w4_d[:, ca].bitcast(FP4X4), lhsT_scale=w4_sc[a][:, c],
+                            out=bank[:, t, :], lhsT=w4_d[:, ca].bitcast(FP4X4), lhsT_scale=wd_sc[:, ca],
                             rhs=g_w[a][:, js].bitcast(FP8X4), rhs_scale=(g_sc, g_sc_low)[a][:, js],
                             start=(a == 0), stop=(a == NPASS - 1),
                         )
@@ -185,8 +185,9 @@ def tile_list_locum_consultant_scores_kernel(
                 flat = banks[t][:]
                 for a in range(NPASS):
                     c = cols(b, t)
+                    ca = slice(H * a + c.start, H * a + c.stop)
                     nc.tensor.matmul_mx(
-                        out=flat, lhsT=w8_d[a][:, c].bitcast(FP8X4), lhsT_scale=wd_sc[4 * a : P, c],
+                        out=flat, lhsT=w8_d[a][:, c].bitcast(FP8X4), lhsT_scale=wd_sc[4:P, ca],
                         rhs=g_w[a][:].bitcast(FP8X4), rhs_scale=g_sc[4 * a : P, :],
                         start=(a == 0), stop=(a == NPASS - 1),
                     )
@@ -256,25 +257,29 @@ def tile_list_locum_consultant_scores_kernel(
         load_w1(0, 1)
         product_w8(0, low)
         product_w8(1, high)
-        c3_sc = gather("c3_sc", U8, v3_sc[:], off3)
+        deal_w4(0)
+        deal_w4(1)
         c3_w = [gather(f"c3_w{a}", U32, v3_w[a], off3) for a in range(NPASS)]
-        c2_sc = gather("c2_sc", U8, v2_sc[:], off2)
+        c3_sc = gather("c3_sc", U8, v3_sc[:], off3)
         load_w1(1, 0)
         load_w1(1, 1)
+        v2_w1 = tile([P, T3], U32, "v2_w1", "stage1")
+        load_words(v2_w1[:], tab2_words[1])
         make_h2(0)
         round_w1(0, 0)
-        product_w4(0, low)
         given_t = tile([P, 4, S], F32, "given_t", "w1_raw00")
         nc.sync.dma_start(out=given_t[:], in_=given.rearrange("(m p) j -> p m j", p=P))
+        product_w4(0, low)
         make_h2(1)
         quantise(h2_w[0][:], h2_sc[0][:], h2_bf[0][:])
-        round_w1(0, 1)
         quantise(h2_w[1][:], h2_sc[1][:], h2_bf[1][:])
-        c2_w0 = gather("c2_w0", U32, v2_w[0], off2, "stage0")
+        round_w1(0, 1)
+        c2_sc = gather("c2_sc", U8, v2_sc[:], off2, "stage0")
+        c2_w0 = gather("c2_w0", U32, v2_w0[:], off2, "w1_bf01")
         make_h1(0, high)
         round_w1(1, 0)
         round_w1(1, 1)
-        c2_w = [c2_w0, gather("c2_w1", U32, v2_w[1], off2, "w1_bf11")]
+        c2_w = [c2_w0, gather("c2_w1", U32, v2_w1[:], off2, "w1_bf11")]
         product_w4(1, low)
         make_h1(1, high)
         e3 = scores(low, c3_w, c3_sc, h2_w, h2_sc)

@@ -280,12 +280,15 @@ def tile_list_locum_consultant_scores_kernel(
         round_w1(1, 0)
         round_w1(1, 1)
         c2_w = [c2_w0, gather("c2_w1", U32, v2_w1[:], off2, "w1_bf11")]
+        e3 = scores(low, c3_w, c3_sc, h2_w, h2_sc)
+        shifted = []
+        for m in range(S2 // P):
+            e3_sb = tile([P, S], F32, f"e3_sb{m}")
+            nc.scalar.copy(out=e3_sb[:], in_=e3[m][:])
+            shifted.append(tile([P, S], F32, f"shifted{m}", "stage1" if m == 0 else None))
+            nc.gpsimd.tensor_tensor(out=shifted[m][:], in0=e3_sb[:], in1=given_t[:, m, :], op=ALU.add)
         product_w4(1, low)
         make_h1(1, high)
-        e3 = scores(low, c3_w, c3_sc, h2_w, h2_sc)
-        shifted = [tile([P, S], F32, f"shifted{m}") for m in range(S2 // P)]
-        for m in range(S2 // P):
-            nc.vector.tensor_tensor(out=shifted[m][:], in0=e3[m][:], in1=given_t[:, m, :], op=ALU.add)
         e2 = scores(high, c2_w, c2_sc, h1_w, h1_sc)
         for m in range(S2 // P):
             res = tile([P, S], F32, f"res{m}")

from contextlib import ExitStack

import concourse.mybir as mybir

K, H, T, S, T3, S2 = 1024, 1024, 2048, 512, 1024, 512
FLOPS = 2 * (3 * K * H * S + 2 * H * S2 * S)

F32 = mybir.dt.float32
BF16 = mybir.dt.bfloat16
I32 = mybir.dt.int32
U32 = mybir.dt.uint32
U16 = mybir.dt.uint16
U8 = mybir.dt.uint8
FP8X4 = mybir.dt.float8_e4m3fn_x4
FP4X4 = mybir.dt.float4_e2m1fn_x4
ALU = mybir.AluOpType
ACT = mybir.ActivationFunctionType

P = 128
PACK = 4
PASS = P * PACK
NPASS = K // PASS
JW = 128


def tile_list_locum_consultant_scores_kernel(
    tc, tab_words, tab_scales, tab2_words, tab2_scales, tab3_words, tab3_scales, offs, offs2, offs3,
    w1, w4_words, w4_scales, w8_words, w8_scales, bias, gain, given, out,
):
    nc = tc.nc
    with ExitStack() as ctx:
        keep = ctx.enter_context(tc.tile_pool(name="keep", bufs=1))
        psum = ctx.enter_context(tc.psum_pool(name="psum", bufs=1))
        low = [psum.tile([P, S], F32, name=f"low{i}") for i in range(4)]
        high = [psum.tile([P, S], F32, name=f"high{i}") for i in range(4)]

        def tile(shape, dtype, name, tag=None):
            return keep.tile(shape, dtype, name=name, tag=tag or name, align_bytes=64)

        def words(ap):
            return ap.rearrange("p n i -> p (n i)").bitcast(I32)

        off1 = keep.tile([P, S // 16], U16, name="off1")
        off2 = keep.tile([P, S2 // 16], U16, name="off2")
        off3 = keep.tile([P, S2 // 16], U16, name="off3")

        v_sc = tile([P, T], U8, "v_sc")
        w_sc = tile([P, NPASS * H], U8, "w_sc")
        v2_sc = tile([P, T3], U8, "v2_sc")
        v3_sc = tile([P, T3], U8, "v3_sc")
        g_sc_low = tile([P, S], U8, "g_sc_low")
        nc.gpsimd.memset(v_sc[:].bitcast(I32), 0)
        nc.vector.memset(w_sc[:].bitcast(I32), 0)
        nc.vector.memset(v3_sc[:].bitcast(I32), 0)
        nc.vector.memset(v2_sc[:].bitcast(I32), 0)
        nc.vector.memset(g_sc_low[:].bitcast(I32), 0)

        def load_planes(queue, dst, scales):
            for q in range(4):
                queue.dma_start(
                    out=dst[32 * q : 32 * q + 8, :].bitcast(I32),
                    in_=scales[:, 4 * q : 4 * q + 4, :].bitcast(I32),
                )

        def load_planes_side_by_side(dst, first, scales):
            for q in range(4):
                rows = dst[32 * q + first : 32 * q + first + 4, :].bitcast(I32)
                nc.sync.dma_start(
                    out=rows.rearrange("r (a n) -> r a n", a=NPASS),
                    in_=scales[:, 4 * q : 4 * q + 4, :].bitcast(I32).rearrange("a r n -> r a n"),
                )

        def lower_plane(dst, src, first):
            nc.sync.dma_start(out=dst[0:100, :].bitcast(I32), in_=src[first : first + 100, :].bitcast(I32))

        v_w = [tile([P, T], U32, f"v_w{a}") for a in range(NPASS)]
        v3_all = tile([P, NPASS * T3], U32, "v3_all")
        v3_w = [v3_all[:, T3 * a : T3 * (a + 1)] for a in range(NPASS)]
        v2_w0 = tile([P, T3], U32, "v2_w0")
        w4_raw = tile([P, H], I32, "w4_raw")
        w8_raw = [tile([P, H], U32, f"w8_raw{a}") for a in range(NPASS)]
        w1_raw = {}
        bias_t = tile([P, 8], F32, "bias_t")
        gain_t = tile([P, 8], F32, "gain_t")

        def load_w1(b, a):
            rows = w1[PASS * a : PASS * (a + 1), PASS * b : PASS * (b + 1)]
            w1_raw[b, a] = tile([P, PACK, PASS], F32, f"w1_raw{b}{a}", (None, "w_sc", "v3_all", "w4_raw")[2 * b + a])
            nc.sync.dma_start(out=w1_raw[b, a][:], in_=rows.rearrange("(p j) c -> p j c", j=PACK))

        def load_words(dst, src):
            nc.sync.dma_start(out=dst.bitcast(I32), in_=words(src))

        def load_vector(dst, src):
            nc.sync.dma_start(out=dst[:].rearrange("p (b t) -> p b t", t=PACK),
                              in_=src.rearrange("(b p t) -> p b t", p=P, t=PACK))

        load_planes(nc.gpsimd, v_sc, tab_scales)
        load_planes(nc.gpsimd, v2_sc, tab2_scales)

        nc.sync.dma_start(off1[:], offs)
        load_words(v_w[0][:], tab_words[0])
        load_planes_side_by_side(w_sc, 4, w8_scales)
        load_words(w8_raw[0][:], w8_words[0])
        load_planes_side_by_side(w_sc, 0, w4_scales)
        load_words(v_w[1][:], tab_words[1])
        load_words(w8_raw[1][:], w8_words[1])
        nc.sync.dma_start(off3[:], offs3)
        load_vector(bias_t, bias)
        load_words(v3_w[0], tab3_words[0])
        load_planes(nc.sync, v3_sc, tab3_scales)
        nc.sync.dma_start(out=w4_raw[:].rearrange("p (a n) -> p a n", a=NPASS),
                          in_=w4_words.bitcast(I32).rearrange("a p n -> p a n"))
        load_words(v3_w[1], tab3_words[1])
        load_vector(gain_t, gain)
        nc.sync.dma_start(off2[:], offs2)
        load_w1(0, 0)
        load_words(v2_w0[:], tab2_words[0])

        g_w = [tile([P, S], U32, f"g_w{a}") for a in range(NPASS)]
        g_sc = tile([P, S], U8, "g_sc")
        w4_d = tile([P, NPASS * H], U16, "w4_d")
        wd_sc = tile([P, NPASS * H], U8, "wd_sc")
        w8_d = [tile([P, H], U32, f"w8_d{a}", f"stage{a}") for a in range(NPASS)]

        def deal_w8(a):
            nc.scalar.copy(
                out=w8_d[a][:].rearrange("p (b t c i) -> p b c t i", b=2, t=PACK, i=4),
                in_=w8_raw[a][:].rearrange("p (b c i t) -> p b c t i", b=2, t=PACK, i=4),
            )

        def deal_w4(a):
            nc.scalar.copy(
                out=w4_d[:, H * a : H * (a + 1)].rearrange("p (b t q) -> p b t q", b=2, t=PACK),
                in_=w4_raw[:, 512 * a : 512 * (a + 1)].bitcast(U16).rearrange("p (b q t) -> p b t q", b=2, t=PACK),
            )

        deal_w8(0)
        deal_w8(1)
        nc.vector.tensor_copy(g_w[0][:], v_w[0][:].indirect(off1[:]))
        nc.vector.tensor_copy(
            out=wd_sc[:].rearrange("p (g t q) -> p g t q", g=4, t=PACK),
            in_=w_sc[:].rearrange("p (g q t) -> p g t q", g=4, t=PACK),
        )
        nc.vector.tensor_copy(g_sc[:], v_sc[:].indirect(off1[:]))
        lower_plane(g_sc_low, g_sc, 4)
        nc.vector.tensor_copy(g_w[1][:], v_w[1][:].indirect(off1[:]))

        def gather(name, dtype, window, off, tag=None):
            picked = tile([P, S2], dtype, name, tag)
            nc.vector.tensor_copy(picked[:], window.indirect(off[:]))
            return picked

        def cols(b, t):
            return slice(PASS * b + P * t, PASS * b + P * (t + 1))

        p4 = {}

        def product_w4(b, banks):
            p4[b] = tile([P, PACK * S], F32, f"p4_{b}", (None, "w4_raw")[b])
            for jc in range(S // JW):
                js = slice(JW * jc, JW * (jc + 1))
                bank = banks[jc][:].rearrange("p (t j) -> p t j", t=PACK)
                for t in range(PACK):
                    for a in range(NPASS):
                        c = cols(b, t)
                        ca = slice(H * a + c.start, H * a + c.stop)
                        nc.tensor.matmul_mx(
                            out=bank[:, t, :], lhsT=w4_d[:, ca].bitcast(FP4X4), lhsT_scale=wd_sc[:, ca],
                            rhs=g_w[a][:, js].bitcast(FP8X4), rhs_scale=(g_sc, g_sc_low)[a][:, js],
                            start=(a == 0), stop=(a == NPASS - 1),
                        )
                nc.scalar.copy(
                    out=p4[b][:, PASS * jc : PASS * (jc + 1)].rearrange("p (j t) -> p j t", t=PACK),
                    in_=bank.rearrange("p t j -> p j t"),
                )

        th = [tile([P, PACK, S], F32, f"th{b}") for b in range(2)]
        h2_bf = [tile([P, PACK * S], BF16, f"h2_bf{b}") for b in range(2)]
        h2_w = [tile([P, S], U32, f"h2_w{b}") for b in range(2)]
        h2_sc = [tile([P, S], U8, f"h2_sc{b}") for b in range(2)]

        def product_w8(b, banks):
            for t in range(PACK):
                flat = banks[t][:]
                for a in range(NPASS):
                    c = cols(b, t)
                    ca = slice(H * a + c.start, H * a + c.stop)
                    nc.tensor.matmul_mx(
                        out=flat, lhsT=w8_d[a][:, c].bitcast(FP8X4), lhsT_scale=wd_sc[4:P, ca],
                        rhs=g_w[a][:].bitcast(FP8X4), rhs_scale=g_sc[4 * a : P, :],
                        start=(a == 0), stop=(a == NPASS - 1),
                    )
                nc.scalar.activation(out=th[b][:, t, :], in_=flat, func=ACT.Tanh,
                                     bias=bias_t[:, PACK * b + t : PACK * b + t + 1])

        def make_h2(b):
            g = gain_t[:, PACK * b : PACK * (b + 1)].unsqueeze(1).unsqueeze(3).to_broadcast([P, S // 4, PACK, 4])
            nc.vector.tensor_tensor(
                out=h2_bf[b][:].rearrange("p (c i t) -> p c t i", i=4, t=PACK),
                in0=th[b][:].rearrange("p t (c i) -> p c t i", i=4),
                in1=g, op=ALU.mult,
            )

        def quantise(codes, scales, src):
            nc.vector.quantize_mx(out=codes.bitcast(FP8X4), scales=scales, in_=src)

        w1_w = [[tile([P, PASS], U32, f"w1_w{b}{a}") for a in range(NPASS)] for b in range(2)]
        w1_sc = [[tile([P, PASS], U8, f"w1_sc{b}{a}") for a in range(NPASS)] for b in range(2)]

        def round_w1(b, a):
            rounded = tile([P, PACK * PASS], BF16, f"w1_bf{b}{a}", "stage0" if (b, a) == (0, 0) else None)
            dst = rounded[:].rearrange("p (t q j) -> p q j t", t=PACK, j=PACK)
            src = w1_raw[b, a][:].rearrange("p j (q t) -> p q j t", t=PACK)
            if (b, a) == (0, 1):
                nc.vector.tensor_copy(out=dst, in_=src)
            else:
                nc.scalar.copy(out=dst, in_=src)
            quantise(w1_w[b][a][:], w1_sc[b][a][:], rounded[:])

        h1_bf = [tile([P, PACK * S], BF16, f"h1_bf{b}") for b in range(2)]
        h1_w = [tile([P, S], U32, f"h1_w{b}") for b in range(2)]
        h1_sc = [tile([P, S], U8, f"h1_sc{b}") for b in range(2)]

        def make_h1(b, banks):
            for jc in range(S // JW):
                js = slice(JW * jc, JW * (jc + 1))
                bank = banks[jc][:].rearrange("p (t j) -> p t j", t=PACK)
                for t in range(PACK):
                    ts = slice(P * t, P * (t + 1))
                    for a in range(NPASS):
                        nc.tensor.matmul_mx(
                            out=bank[:, t, :], lhsT=w1_w[b][a][:, ts].bitcast(FP8X4), lhsT_scale=w1_sc[b][a][:, ts],
                            rhs=g_w[a][:, js].bitcast(FP8X4), rhs_scale=g_sc[4 * a : P, js],
                            start=(a == 0), stop=(a == NPASS - 1),
                        )
                part = slice(PASS * jc, PASS * (jc + 1))
                nc.vector.tensor_tensor(
                    out=h1_bf[b][:, part].rearrange("p (j t) -> p j t", t=PACK),
                    in0=bank.rearrange("p t j -> p j t"),
                    in1=p4[b][:, part].rearrange("p (j t) -> p j t", t=PACK),
                    op=ALU.max,
                )
            quantise(h1_w[b][:], h1_sc[b][:], h1_bf[b][:])

        def scores(banks, c_w, c_sc, h_w, h_sc):
            for b in range(2):
                for m in range(S2 // P):
                    ms = slice(P * m, P * (m + 1))
                    nc.tensor.matmul_mx(
                        out=banks[m][:], lhsT=c_w[b][:, ms].bitcast(FP8X4), lhsT_scale=c_sc[4 * b : P, ms],
                        rhs=h_w[b][:].bitcast(FP8X4), rhs_scale=h_sc[b][:],
                        start=(b == 0), stop=(b == 1),
                    )
            return banks

        load_w1(0, 1)
        product_w8(0, low)
        product_w8(1, high)
        deal_w4(0)
        deal_w4(1)
        c3_w = [gather(f"c3_w{a}", U32, v3_w[a], off3) for a in range(NPASS)]
        c3_sc = gather("c3_sc", U8, v3_sc[:], off3)
        load_w1(1, 0)
        load_w1(1, 1)
        v2_w1 = tile([P, T3], U32, "v2_w1", "stage1")
        load_words(v2_w1[:], tab2_words[1])
        make_h2(0)
        round_w1(0, 0)
        given_t = tile([P, 4, S], F32, "given_t", "w1_raw00")
        nc.sync.dma_start(out=given_t[:], in_=given.rearrange("(m p) j -> p m j", p=P))
        product_w4(0, low)
        make_h2(1)
        quantise(h2_w[0][:], h2_sc[0][:], h2_bf[0][:])
        quantise(h2_w[1][:], h2_sc[1][:], h2_bf[1][:])
        round_w1(0, 1)
        c2_sc = gather("c2_sc", U8, v2_sc[:], off2, "stage0")
        c2_w0 = gather("c2_w0", U32, v2_w0[:], off2, "w1_bf01")
        make_h1(0, high)
        round_w1(1, 0)
        round_w1(1, 1)
        c2_w = [c2_w0, gather("c2_w1", U32, v2_w1[:], off2, "w1_bf11")]
        e3 = scores(low, c3_w, c3_sc, h2_w, h2_sc)
        shifted = []
        for m in range(S2 // P):
            e3_sb = tile([P, S], F32, f"e3_sb{m}")
            nc.scalar.copy(out=e3_sb[:], in_=e3[m][:])
            shifted.append(tile([P, S], F32, f"shifted{m}", "stage1" if m == 0 else None))
            nc.gpsimd.tensor_tensor(out=shifted[m][:], in0=e3_sb[:], in1=given_t[:, m, :], op=ALU.add)
        product_w4(1, low)
        make_h1(1, high)
        e2 = scores(high, c2_w, c2_sc, h1_w, h1_sc)
        for m in range(S2 // P):
            res = tile([P, S], F32, f"res{m}")
            nc.vector.tensor_tensor(out=res[:], in0=e2[m][:], in1=shifted[m][:], op=ALU.min)
            nc.sync.dma_start(out=out[P * m : P * (m + 1), :], in_=res[:])
